import numpy as np
import ml_dtypes


def mxq(x, axis, fmt="e4m3"):
    dtype, down = {"e4m3": (ml_dtypes.float8_e4m3fn, 7), "e5m2": (ml_dtypes.float8_e5m2, 14)}[fmt]
    v = np.moveaxis(np.asarray(x, np.float32).astype(ml_dtypes.bfloat16).astype(np.float64), axis, -1)
    blocks = v.reshape(v.shape[:-1] + (-1, 32))
    amax = np.abs(blocks).max(-1, keepdims=True)
    byte = np.maximum(np.where(amax > 0, np.frexp(amax)[1] - 1 + 127, 0) - down, 1)
    scale = np.exp2(byte - 127.0)
    codes = (blocks / scale).astype(np.float32).astype(dtype).astype(np.float64)
    return np.moveaxis((codes * scale).reshape(v.shape), -1, axis)


WIDE = False


def mx_kscale(k):
    if not WIDE:
        return np.ones(k)
    levels = np.array([10, -10, 5, -5, 0])
    if k % 512:
        return np.exp2(np.random.permutation(np.resize(levels, k // 32))).repeat(32)
    a = np.empty((k // 512, 16))
    for p in range(k // 512):
        a[p, :8] = np.random.permutation(np.resize(levels, 8))
        for g in range(8):
            far = levels[np.abs(levels - a[p, g]) >= 10]
            a[p, g + 8] = far[np.random.randint(len(far))]
    return np.exp2(a.ravel()).repeat(32)


def f64(x):
    return np.asarray(x).astype(np.float64)


def striped(idx):
    return np.tile(idx.reshape(-1, 16).T, (8, 1)).astype(np.uint16)


def unstriped(offs):
    return offs[:16].T.reshape(-1).astype(np.int64)


def striped8(idx):
    return np.concatenate([x.reshape(-1, 16).T for x in idx]).astype(np.uint16)


def runs(offs, k):
    lists = np.stack([offs[16 * r : 16 * r + 16].T.reshape(-1) for r in range(8)]).astype(np.int64)
    return lists[np.arange(k) % 512 // 64]


def pack_weight(w):
    k, n = w.shape
    w = f64(np.asarray(w, np.float32).astype(ml_dtypes.bfloat16)).reshape(k // 32, 32, n)
    amax = np.abs(w).max(1)
    byte = np.clip(np.where(amax > 0, np.frexp(amax)[1] - 1 + 127 - 7, 1), 1, 254)
    scaled = (w * np.exp2(127.0 - byte)[:, None, :]).reshape(k, n).astype(np.float32)
    words = np.ascontiguousarray(scaled.reshape(k // 512, 128, 4, n).transpose(0, 1, 3, 2)).astype(ml_dtypes.float8_e4m3fn).view(np.uint8)
    return words, np.ascontiguousarray(byte.astype(np.uint8).reshape(k // 512, 16, n))


def unpack_weight(words, scales):
    g, p, n, _ = words.shape
    vals = np.ascontiguousarray(words).view(ml_dtypes.float8_e4m3fn).astype(np.float64) * np.repeat(np.exp2(scales.astype(np.float64) - 127.0), 8, axis=1)[..., None]
    return vals.transpose(0, 1, 3, 2).reshape(g * 512, n)


K, T, S, N, H = 512, 2048, 512, 512, 512


def setup_inputs():
    n = np.random.standard_normal
    s = mx_kscale(K)[:, None]
    u = mx_kscale(H)
    packed_xT = pack_weight(n((K, T)) * s)
    return {
        "x_words": packed_xT[0],
        "x_scales": packed_xT[1],
        "w1": (n((K, H)) / np.sqrt(K) / s).astype(np.float32),
        "gn": (np.random.uniform(0.5, 1.5, (H, 1)) * u[:, None]).astype(np.float32),
        "w2": (n((H, N)) / np.sqrt(H) / u[:, None]).astype(np.float32),
        "w3": (n((K, N)) / np.sqrt(K) / s).astype(np.float32),
        "offs": striped(np.random.permutation(T)[:S]),
        "n1": striped8(np.stack([np.random.permutation(S) for _ in range(8)])),
        "n2": striped8(np.stack([np.random.permutation(S) for _ in range(8)])),
        "two": striped(np.random.permutation(T)[:S]),
        "n3": striped8(np.stack([np.random.permutation(S) for _ in range(8)])),
        "n4": striped8(np.stack([np.random.permutation(S) for _ in range(8)])),
        "n5": striped8(np.stack([np.random.permutation(S) for _ in range(8)])),
    }


def reference(x_words, x_scales, w1, gn, w2, w3, offs, n1, n2, two, n3, n4, n5):
    x_two = unpack_weight(x_words, x_scales)[:, unstriped(two)]
    d = mxq(f64(w3), 0, "e4m3").T @ x_two
    xq = unpack_weight(x_words, x_scales)[:, unstriped(offs)]
    y = mxq(f64(w1), 0, "e4m3").T @ xq
    sq = (y) ** 2
    z = f64(gn) * ((y[np.arange(H)[:, None], runs(n2, H)]) / (np.sqrt(sq + sq[np.arange(H)[:, None], runs(n1, H)] + 0.25)))
    h = mxq(f64(w2), 0, "e4m3").T @ mxq(z, 0, "e4m3")
    return d * (h[np.arange(N)[:, None], runs(n3, N)] - h) + 0.5 * ((d[np.arange(N)[:, None], runs(n5, N)]) * (h[np.arange(N)[:, None], runs(n4, N)] - h))

@@ -1,0 +1,164 @@
+from contextlib import ExitStack
+
+import concourse.mybir as mybir
+
+F32 = mybir.dt.float32
+BF16 = mybir.dt.bfloat16
+I32 = mybir.dt.int32
+U32 = mybir.dt.uint32
+U16 = mybir.dt.uint16
+U8 = mybir.dt.uint8
+FP8X4 = mybir.dt.float8_e4m3fn_x4
+ACT = mybir.ActivationFunctionType
+ALU = mybir.AluOpType
+
+P = 128
+PACK = 4
+T = 2048
+S = 512
+HALF = S // 2
+FLOPS = 3 * 2 * 512 * 512 * 512
+
+
+def tile_picked_lateflowbrms_none_p_kernel(
+    tc, x_words, x_scales, w1, gn, w2, w3, offs, n1, n2, two, n3, n4, n5, out
+):
+    nc = tc.nc
+    with ExitStack() as ctx:
+        keep = ctx.enter_context(tc.tile_pool(name="keep", bufs=1))
+        psum = ctx.enter_context(tc.psum_pool(name="psum", bufs=1))
+
+        def load_list(src, name):
+            tile = keep.tile([P, S // 16], U16, name=name)
+            nc.sync.dma_start(tile[:], src)
+            return tile
+
+        def load_weight(src, name):
+            tile = keep.tile([P, PACK, S], F32, name=name)
+            nc.sync.dma_start(out=tile[:], in_=src.rearrange("(p j) c -> p j c", j=PACK))
+            return tile
+
+        xs = keep.tile([P, T], U8, name="xs", align_bytes=64)
+        nc.vector.memset(xs[:].bitcast(I32), 0)
+        warm_in = keep.tile([P, 1], F32, name="warm_in")
+        warm_out = keep.tile([P, 1], F32, name="warm_out")
+        nc.vector.memset(warm_in[:], 1.0)
+        offs_t = load_list(offs, "offs_t")
+        for q in range(4):
+            nc.scalar.dma_start(out=xs[32 * q : 32 * q + 4, :].bitcast(I32), in_=x_scales[0, 4 * q : 4 * q + 4, :].bitcast(I32))
+        nc.scalar.activation(out=warm_out[:], in_=warm_in[:], func=ACT.Abs_reciprocal_sqrt)
+        xw = keep.tile([P, T], I32, name="xw", align_bytes=64)
+        nc.sync.dma_start(out=xw[:], in_=x_words[0].rearrange("p n t -> p (n t)").bitcast(I32))
+        two_t = load_list(two, "two_t")
+        w1_raw = load_weight(w1, "w1_raw")
+        gn_t = keep.tile([P, PACK], F32, name="gn_t")
+        nc.sync.dma_start(out=gn_t[:], in_=gn.rearrange("(p t) o -> p (t o)", t=PACK))
+        n1_t = load_list(n1, "n1_t")
+        n2_t = load_list(n2, "n2_t")
+        w3_raw = load_weight(w3, "w3_raw")
+        w2_raw = load_weight(w2, "w2_raw")
+        n5_t = load_list(n5, "n5_t")
+        n3_t = load_list(n3, "n3_t")
+        n4_t = load_list(n4, "n4_t")
+
+        sq_win = [keep.tile([P, 2 * S], F32, name="sq_win%d" % t) for t in range(PACK)]
+        y_win = [keep.tile([P, 2 * S], F32, name="y_win%d" % t) for t in range(PACK)]
+        d_win = [keep.tile([P, 2 * S], F32, name="d_win%d" % t) for t in range(PACK)]
+        for t in range(PACK):
+            nc.gpsimd.memset(sq_win[t][:, S:], 0.0)
+            nc.gpsimd.memset(d_win[t][:, S:], 0.0)
+
+        def pick(lst, name):
+            words = keep.tile([P, S], U32, name=name + "_words", align_bytes=64)
+            scales = keep.tile([P, S], U8, name=name + "_scales", align_bytes=64)
+            nc.vector.tensor_copy(out=scales[:], in_=xs[:].indirect(lst[:]))
+            nc.vector.tensor_copy(out=words[:], in_=xw[:].bitcast(U32).indirect(lst[:]))
+            return words, scales
+
+        def quantise_weight(raw, name):
+            grouped = keep.tile([P, PACK * S], BF16, name=name + "_grouped", align_bytes=64)
+            nc.scalar.copy(
+                out=grouped[:].rearrange("p (t m j) -> p m j t", t=PACK, j=PACK),
+                in_=raw[:].rearrange("p j (m t) -> p m j t", t=PACK),
+            )
+            codes = keep.tile([P, S], U32, name=name + "_codes", align_bytes=64)
+            scales = keep.tile([P, S], U8, name=name + "_sc", align_bytes=64)
+            nc.vector.quantize_mx(out=codes[:].bitcast(FP8X4), scales=scales[:], in_=grouped[:])
+            return codes, scales
+
+        def product(acc, w, t, x, cols):
+            m = slice(P * t, P * (t + 1))
+            nc.tensor.matmul_mx(
+                out=acc, lhsT=w[0][:, m].bitcast(FP8X4), lhsT_scale=w[1][:, m],
+                rhs=x[0][:, cols].bitcast(FP8X4), rhs_scale=x[1][:, cols], start=True, stop=True,
+            )
+
+        xq = pick(offs_t, "xq")
+        x2 = pick(two_t, "x2")
+        w1q = quantise_weight(w1_raw, "w1")
+        whole = slice(0, S)
+
+        s = keep.tile([P, PACK, S], F32, name="s")
+        r = keep.tile([P, PACK, S], F32, name="r")
+        z = keep.tile([P, PACK, S], F32, name="z")
+        for t in range(PACK):
+            y = psum.tile([P, S], F32, name="y%d" % t, tag="yh%d" % t)
+            product(y[:], w1q, t, xq, whole)
+            nc.scalar.activation(out=sq_win[t][:, :S], in_=y[:], func=ACT.Square)
+            nc.scalar.activation(out=y_win[t][:, S:], in_=y[:], func=ACT.Square)
+            nc.vector.tensor_tensor(out=s[:, t, :], in0=sq_win[t][:].indirect(n1_t[:]), in1=y_win[t][:, S:], op=ALU.add)
+            nc.scalar.activation(out=y_win[t][:, :S], in_=y[:], func=ACT.Copy, scale=gn_t[:, t : t + 1])
+        for t in range(PACK):
+            nc.scalar.activation(out=r[:, t, :], in_=s[:, t, :], func=ACT.Abs_reciprocal_sqrt, bias=0.25)
+
+        w3q = quantise_weight(w3_raw, "w3")
+        w2q = quantise_weight(w2_raw, "w2")
+        d = []
+        for t in range(PACK):
+            d.append(psum.tile([P, S], F32, name="d%d" % t, tag="d%d" % t))
+            product(d[t][:], w3q, t, x2, whole)
+            nc.scalar.activation(out=d_win[t][:, :S], in_=d[t][:], func=ACT.Copy, scale=0.5)
+
+        zg = keep.tile([P, S, PACK], BF16, name="zg", align_bytes=64)
+        zc = keep.tile([P, S], U32, name="zc", align_bytes=64)
+        zs = keep.tile([P, S], U8, name="zs", align_bytes=64)
+        h = [psum.tile([P, S], F32, name="h%d" % t, tag="yh%d" % t) for t in range(PACK)]
+        h_plain = keep.tile([P, PACK, S], F32, name="h_plain")
+        for half in range(2):
+            cols = slice(HALF * half, HALF * (half + 1))
+            for t in range(PACK):
+                nc.vector.tensor_tensor(
+                    out=z[:, t, cols], in0=y_win[t][:].indirect(n2_t[:, 16 * half : 16 * half + 16]), in1=r[:, t, cols], op=ALU.mult
+                )
+            dst = zg[:, cols, :].rearrange("p (c i) t -> p c t i", i=4)
+            src = z[:, :, cols].rearrange("p t (c i) -> p c t i", i=4)
+            if half == 0:
+                nc.scalar.copy(out=dst, in_=src)
+            else:
+                nc.vector.tensor_copy(out=dst, in_=src)
+        for half in range(2):
+            cols = slice(HALF * half, HALF * (half + 1))
+            nc.vector.quantize_mx(out=zc[:, cols].bitcast(FP8X4), scales=zs[:, cols], in_=zg[:, cols, :].rearrange("p c t -> p (c t)"))
+            for t in range(PACK):
+                product(h[t][:, cols], w2q, t, (zc, zs), cols)
+                nc.scalar.copy(out=sq_win[t][:, cols], in_=h[t][:, cols])
+                nc.scalar.copy(out=h_plain[:, t, cols], in_=h[t][:, cols])
+
+        d5_first = keep.tile([P, S], F32, name="d5_first")
+        nc.vector.tensor_copy(out=d5_first[:], in_=d_win[0][:].indirect(n5_t[:]))
+        a = keep.tile([P, PACK, S], F32, name="a")
+        b = keep.tile([P, PACK, S], F32, name="b")
+        c = keep.tile([P, PACK, S], F32, name="c")
+        e = keep.tile([P, PACK, S], F32, name="e")
+        res = keep.tile([P, PACK, S], F32, name="res")
+        out_rows = out.rearrange("(p t) j -> p t j", t=PACK)
+        for t in range(PACK):
+            nc.vector.tensor_tensor(out=b[:, t, :], in0=sq_win[t][:].indirect(n4_t[:]), in1=h_plain[:, t, :], op=ALU.subtract)
+            nc.vector.tensor_tensor(out=a[:, t, :], in0=sq_win[t][:].indirect(n3_t[:]), in1=h_plain[:, t, :], op=ALU.subtract)
+            if t == 0:
+                nc.vector.tensor_tensor(out=c[:, t, :], in0=d5_first[:], in1=b[:, t, :], op=ALU.mult)
+            else:
+                nc.vector.tensor_tensor(out=c[:, t, :], in0=d_win[t][:].indirect(n5_t[:]), in1=b[:, t, :], op=ALU.mult)
+            nc.vector.tensor_tensor(out=e[:, t, :], in0=d[t][:], in1=a[:, t, :], op=ALU.mult)
+            nc.vector.tensor_tensor(out=res[:, t, :], in0=c[:, t, :], in1=e[:, t, :], op=ALU.add)
+            nc.sync.dma_start(out=out_rows[:, t, :], in_=res[:, t, :])

@@ -1,6 +1,7 @@
 from contextlib import ExitStack
 
 import concourse.mybir as mybir
+from concourse.masks import make_identity
 
 F32 = mybir.dt.float32
 BF16 = mybir.dt.bfloat16
@@ -38,127 +39,167 @@ def tile_picked_lateflowbrms_none_p_kernel(
             nc.sync.dma_start(out=tile[:], in_=src.rearrange("(p j) c -> p j c", j=PACK))
             return tile
 
+        def load_columns(src, cols, name):
+            tile = keep.tile([P, PACK, cols.stop - cols.start], F32, name=name)
+            nc.sync.dma_start(out=tile[:], in_=src[:, cols].rearrange("(p j) c -> p j c", j=PACK))
+            return tile
+
+        halves = [slice(0, HALF), slice(HALF, S)]
         xs = keep.tile([P, T], U8, name="xs", align_bytes=64)
-        nc.vector.memset(xs[:].bitcast(I32), 0)
+        nc.gpsimd.memset(xs[:].bitcast(I32), 0)
         warm_in = keep.tile([P, 1], F32, name="warm_in")
         warm_out = keep.tile([P, 1], F32, name="warm_out")
         nc.vector.memset(warm_in[:], 1.0)
+        nc.scalar.activation(out=warm_out[:], in_=warm_in[:], func=ACT.Abs_reciprocal_sqrt)
+        w1_raw = [load_columns(w1, halves[0], "w1_raw0")]
         offs_t = load_list(offs, "offs_t")
         for q in range(4):
-            nc.scalar.dma_start(out=xs[32 * q : 32 * q + 4, :].bitcast(I32), in_=x_scales[0, 4 * q : 4 * q + 4, :].bitcast(I32))
-        nc.scalar.activation(out=warm_out[:], in_=warm_in[:], func=ACT.Abs_reciprocal_sqrt)
+            nc.sync.dma_start(out=xs[32 * q : 32 * q + 4, :].bitcast(I32), in_=x_scales[0, 4 * q : 4 * q + 4, :].bitcast(I32))
+        w1_raw.append(load_columns(w1, halves[1], "w1_raw1"))
         xw = keep.tile([P, T], I32, name="xw", align_bytes=64)
         nc.sync.dma_start(out=xw[:], in_=x_words[0].rearrange("p n t -> p (n t)").bitcast(I32))
         two_t = load_list(two, "two_t")
-        w1_raw = load_weight(w1, "w1_raw")
+        n1_t = load_list(n1, "n1_t")
         gn_t = keep.tile([P, PACK], F32, name="gn_t")
         nc.sync.dma_start(out=gn_t[:], in_=gn.rearrange("(p t) o -> p (t o)", t=PACK))
-        n1_t = load_list(n1, "n1_t")
         n2_t = load_list(n2, "n2_t")
-        w3_raw = load_weight(w3, "w3_raw")
         w2_raw = load_weight(w2, "w2_raw")
-        n5_t = load_list(n5, "n5_t")
-        n3_t = load_list(n3, "n3_t")
+        w3_raw = load_weight(w3, "w3_raw")
         n4_t = load_list(n4, "n4_t")
+        n3_t = load_list(n3, "n3_t")
+        n5_t = load_list(n5, "n5_t")
 
         sq_win = [keep.tile([P, 2 * S], F32, name="sq_win%d" % t) for t in range(PACK)]
         y_win = [keep.tile([P, 2 * S], F32, name="y_win%d" % t) for t in range(PACK)]
         d_win = [keep.tile([P, 2 * S], F32, name="d_win%d" % t) for t in range(PACK)]
         for t in range(PACK):
             nc.gpsimd.memset(sq_win[t][:, S:], 0.0)
-            nc.gpsimd.memset(d_win[t][:, S:], 0.0)
+        ident = keep.tile([P, P], F32, name="ident")
+        make_identity(nc, ident[:])
 
-        def pick(lst, name):
-            words = keep.tile([P, S], U32, name=name + "_words", align_bytes=64)
-            scales = keep.tile([P, S], U8, name=name + "_scales", align_bytes=64)
+        def pick_scales(lst, name):
+            scales = keep.tile([P, S], U8, name=name, align_bytes=64)
             nc.vector.tensor_copy(out=scales[:], in_=xs[:].indirect(lst[:]))
-            nc.vector.tensor_copy(out=words[:], in_=xw[:].bitcast(U32).indirect(lst[:]))
-            return words, scales
+            return scales
 
-        def quantise_weight(raw, name):
-            grouped = keep.tile([P, PACK * S], BF16, name=name + "_grouped", align_bytes=64)
-            nc.scalar.copy(
-                out=grouped[:].rearrange("p (t m j) -> p m j t", t=PACK, j=PACK),
+        def pick_words(lst, name):
+            words = keep.tile([P, S], U32, name=name, align_bytes=64)
+            nc.vector.tensor_copy(out=words[:], in_=xw[:].bitcast(U32).indirect(lst[:]))
+            return words
+
+        def deal(copy, grouped, raw, first):
+            n = raw.shape[2] // PACK
+            copy(
+                out=grouped[:].rearrange("p (t m j) -> p m j t", t=PACK, j=PACK)[:, first : first + n],
                 in_=raw[:].rearrange("p j (m t) -> p m j t", t=PACK),
             )
+
+        def quantise(grouped, name):
             codes = keep.tile([P, S], U32, name=name + "_codes", align_bytes=64)
             scales = keep.tile([P, S], U8, name=name + "_sc", align_bytes=64)
             nc.vector.quantize_mx(out=codes[:].bitcast(FP8X4), scales=scales[:], in_=grouped[:])
             return codes, scales
 
-        def product(acc, w, t, x, cols):
+        def product(acc, w, t, x, cols=slice(0, S)):
             m = slice(P * t, P * (t + 1))
             nc.tensor.matmul_mx(
-                out=acc, lhsT=w[0][:, m].bitcast(FP8X4), lhsT_scale=w[1][:, m],
+                out=acc[:, cols], lhsT=w[0][:, m].bitcast(FP8X4), lhsT_scale=w[1][:, m],
                 rhs=x[0][:, cols].bitcast(FP8X4), rhs_scale=x[1][:, cols], start=True, stop=True,
             )
 
-        xq = pick(offs_t, "xq")
-        x2 = pick(two_t, "x2")
-        w1q = quantise_weight(w1_raw, "w1")
-        whole = slice(0, S)
+        xq_scales = pick_scales(offs_t, "xq_scales")
+        x2_scales = pick_scales(two_t, "x2_scales")
+        w1_grouped = keep.tile([P, PACK * S], BF16, name="w1_grouped", align_bytes=64)
+        for half in range(2):
+            deal(nc.scalar.copy, w1_grouped, w1_raw[half], half * P // 2)
+        w1q = quantise(w1_grouped, "w1")
+        xq_words = keep.tile([P, S], U32, name="xq_words", align_bytes=64)
+        for half in range(2):
+            nc.vector.tensor_copy(out=xq_words[:, halves[half]], in_=xw[:].bitcast(U32).indirect(offs_t[:, 16 * half : 16 * half + 16]))
+        xq = (xq_words, xq_scales)
+        x2 = (pick_words(two_t, "x2_words"), x2_scales)
 
         s = keep.tile([P, PACK, S], F32, name="s")
         r = keep.tile([P, PACK, S], F32, name="r")
         z = keep.tile([P, PACK, S], F32, name="z")
+        y = []
         for t in range(PACK):
-            y = psum.tile([P, S], F32, name="y%d" % t, tag="yh%d" % t)
-            product(y[:], w1q, t, xq, whole)
-            nc.scalar.activation(out=sq_win[t][:, :S], in_=y[:], func=ACT.Square)
-            nc.scalar.activation(out=y_win[t][:, S:], in_=y[:], func=ACT.Square)
+            bank = psum.tile([P, S], F32, name="y%d" % t, tag="yd%d" % t)
+            if t == 0:
+                early = psum.tile([P, S], F32, name="y_early", tag="h0")
+                y.append([(early, halves[0]), (bank, halves[1])])
+            else:
+                y.append([(bank, slice(0, S))])
+            for acc, cols in y[t]:
+                product(acc, w1q, t, xq, cols)
+                nc.scalar.activation(out=sq_win[t][:, cols], in_=acc[:, cols], func=ACT.Square)
+                nc.scalar.activation(out=y_win[t][:, S:][:, cols], in_=acc[:, cols], func=ACT.Square)
             nc.vector.tensor_tensor(out=s[:, t, :], in0=sq_win[t][:].indirect(n1_t[:]), in1=y_win[t][:, S:], op=ALU.add)
-            nc.scalar.activation(out=y_win[t][:, :S], in_=y[:], func=ACT.Copy, scale=gn_t[:, t : t + 1])
         for t in range(PACK):
+            for acc, cols in y[t]:
+                nc.scalar.activation(out=y_win[t][:, cols], in_=acc[:, cols], func=ACT.Copy, scale=gn_t[:, t : t + 1])
             nc.scalar.activation(out=r[:, t, :], in_=s[:, t, :], func=ACT.Abs_reciprocal_sqrt, bias=0.25)
+            nc.vector.tensor_tensor(out=z[:, t, :], in0=y_win[t][:].indirect(n2_t[:]), in1=r[:, t, :], op=ALU.mult)
 
-        w3q = quantise_weight(w3_raw, "w3")
-        w2q = quantise_weight(w2_raw, "w2")
-        d = []
+        w2_grouped = keep.tile([P, PACK * S], BF16, name="w2_grouped", align_bytes=64)
+        deal(nc.scalar.copy, w2_grouped, w2_raw, 0)
+        zg = keep.tile([P, PACK * S], BF16, name="zg", align_bytes=64)
+        zg_view = zg[:].rearrange("p (c i t) -> p c t i", i=4, t=PACK)
+        z_view = z[:].rearrange("p t (c i) -> p c t i", i=4)
+        nc.vector.tensor_copy(out=zg_view[:, :80], in_=z_view[:, :80])
+        nc.scalar.copy(out=zg_view[:, 80:], in_=z_view[:, 80:])
+        w2q = quantise(w2_grouped, "w2")
+        zq = quantise(zg, "z")
+        deal(nc.vector.tensor_copy, zg, w3_raw, 0)
+        w3q = quantise(zg, "w3")
+
+        h, d = [], []
         for t in range(PACK):
-            d.append(psum.tile([P, S], F32, name="d%d" % t, tag="d%d" % t))
-            product(d[t][:], w3q, t, x2, whole)
+            h.append(psum.tile([P, S], F32, name="h%d" % t, tag="h%d" % t))
+            product(h[t], w2q, t, zq)
+        for t in range(PACK):
+            d.append(psum.tile([P, S], F32, name="d%d" % t, tag="yd%d" % t))
+            product(d[t], w3q, t, x2)
+        for t in range(PACK):
+            nc.scalar.copy(out=sq_win[t][:, :S], in_=h[t][:])
+            nc.scalar.copy(out=d_win[t][:, S:], in_=h[t][:])
             nc.scalar.activation(out=d_win[t][:, :S], in_=d[t][:], func=ACT.Copy, scale=0.5)
 
-        zg = keep.tile([P, S, PACK], BF16, name="zg", align_bytes=64)
-        zc = keep.tile([P, S], U32, name="zc", align_bytes=64)
-        zs = keep.tile([P, S], U8, name="zs", align_bytes=64)
-        h = [psum.tile([P, S], F32, name="h%d" % t, tag="yh%d" % t) for t in range(PACK)]
-        h_plain = keep.tile([P, PACK, S], F32, name="h_plain")
-        for half in range(2):
-            cols = slice(HALF * half, HALF * (half + 1))
-            for t in range(PACK):
-                nc.vector.tensor_tensor(
-                    out=z[:, t, cols], in0=y_win[t][:].indirect(n2_t[:, 16 * half : 16 * half + 16]), in1=r[:, t, cols], op=ALU.mult
-                )
-            dst = zg[:, cols, :].rearrange("p (c i) t -> p c t i", i=4)
-            src = z[:, :, cols].rearrange("p t (c i) -> p c t i", i=4)
-            if half == 0:
-                nc.scalar.copy(out=dst, in_=src)
-            else:
-                nc.vector.tensor_copy(out=dst, in_=src)
-        for half in range(2):
-            cols = slice(HALF * half, HALF * (half + 1))
-            nc.vector.quantize_mx(out=zc[:, cols].bitcast(FP8X4), scales=zs[:, cols], in_=zg[:, cols, :].rearrange("p c t -> p (c t)"))
-            for t in range(PACK):
-                product(h[t][:, cols], w2q, t, (zc, zs), cols)
-                nc.scalar.copy(out=sq_win[t][:, cols], in_=h[t][:, cols])
-                nc.scalar.copy(out=h_plain[:, t, cols], in_=h[t][:, cols])
-
-        d5_first = keep.tile([P, S], F32, name="d5_first")
-        nc.vector.tensor_copy(out=d5_first[:], in_=d_win[0][:].indirect(n5_t[:]))
         a = keep.tile([P, PACK, S], F32, name="a")
         b = keep.tile([P, PACK, S], F32, name="b")
         c = keep.tile([P, PACK, S], F32, name="c")
         e = keep.tile([P, PACK, S], F32, name="e")
         res = keep.tile([P, PACK, S], F32, name="res")
         out_rows = out.rearrange("(p t) j -> p t j", t=PACK)
-        for t in range(PACK):
-            nc.vector.tensor_tensor(out=b[:, t, :], in0=sq_win[t][:].indirect(n4_t[:]), in1=h_plain[:, t, :], op=ALU.subtract)
-            nc.vector.tensor_tensor(out=a[:, t, :], in0=sq_win[t][:].indirect(n3_t[:]), in1=h_plain[:, t, :], op=ALU.subtract)
-            if t == 0:
-                nc.vector.tensor_tensor(out=c[:, t, :], in0=d5_first[:], in1=b[:, t, :], op=ALU.mult)
-            else:
-                nc.vector.tensor_tensor(out=c[:, t, :], in0=d_win[t][:].indirect(n5_t[:]), in1=b[:, t, :], op=ALU.mult)
-            nc.vector.tensor_tensor(out=e[:, t, :], in0=d[t][:], in1=a[:, t, :], op=ALU.mult)
-            nc.vector.tensor_tensor(out=res[:, t, :], in0=c[:, t, :], in1=e[:, t, :], op=ALU.add)
+
+        def finish(t, cols):
+            nc.vector.tensor_tensor(out=res[:, t, cols], in0=c[:, t, cols], in1=e[:, t, cols], op=ALU.add)
+            nc.sync.dma_start(out=out_rows[:, t, cols], in_=res[:, t, cols])
+
+        def finish_on_tensor(t):
+            turned = psum.tile([P, S], F32, name="turned%d" % t, tag="h%d" % t)
+            for k in range(PACK):
+                cols = slice(P * k, P * (k + 1))
+                nc.tensor.matmul(out=turned[:, cols], lhsT=c[:, t, cols], rhs=ident[:], is_transpose=True, start=True, stop=False)
+                nc.tensor.matmul(out=turned[:, cols], lhsT=e[:, t, cols], rhs=ident[:], is_transpose=True, start=False, stop=True)
+            nc.scalar.copy(out=a[:, t, :], in_=turned[:])
+            back = psum.tile([P, S], F32, name="back%d" % t, tag="yd%d" % t)
+            for k in range(PACK):
+                cols = slice(P * k, P * (k + 1))
+                nc.tensor.transpose(back[:, cols], a[:, t, cols], ident[:])
+            nc.scalar.copy(out=res[:, t, :], in_=back[:])
             nc.sync.dma_start(out=out_rows[:, t, :], in_=res[:, t, :])
+
+        for t in range(PACK):
+            nc.vector.tensor_tensor(out=b[:, t, :], in0=sq_win[t][:].indirect(n4_t[:]), in1=d_win[t][:, S:], op=ALU.subtract)
+            nc.vector.tensor_tensor(out=a[:, t, :], in0=sq_win[t][:].indirect(n3_t[:]), in1=d_win[t][:, S:], op=ALU.subtract)
+            if t < PACK - 1:
+                nc.vector.tensor_tensor(out=c[:, t, :], in0=d_win[t][:].indirect(n5_t[:]), in1=b[:, t, :], op=ALU.mult)
+                nc.vector.tensor_tensor(out=e[:, t, :], in0=d[t][:], in1=a[:, t, :], op=ALU.mult)
+                finish_on_tensor(t)
+        t = PACK - 1
+        nc.vector.tensor_tensor(out=c[:, t, halves[0]], in0=d_win[t][:].indirect(n5_t[:, 0:16]), in1=b[:, t, halves[0]], op=ALU.mult)
+        nc.vector.tensor_tensor(out=e[:, t, :], in0=d[t][:], in1=a[:, t, :], op=ALU.mult)
+        nc.vector.tensor_tensor(out=c[:, t, halves[1]], in0=d_win[t][:].indirect(n5_t[:, 16:32]), in1=b[:, t, halves[1]], op=ALU.mult)
+        finish(t, halves[0])
+        finish(t, halves[1])

@@ -51,14 +51,14 @@ def tile_picked_lateflowbrms_none_p_kernel(
         warm_out = keep.tile([P, 1], F32, name="warm_out")
         nc.vector.memset(warm_in[:], 1.0)
         nc.scalar.activation(out=warm_out[:], in_=warm_in[:], func=ACT.Abs_reciprocal_sqrt)
-        w1_raw = [load_columns(w1, halves[0], "w1_raw0")]
         offs_t = load_list(offs, "offs_t")
+        two_t = load_list(two, "two_t")
+        w1_raw = [load_columns(w1, halves[0], "w1_raw0")]
         for q in range(4):
             nc.sync.dma_start(out=xs[32 * q : 32 * q + 4, :].bitcast(I32), in_=x_scales[0, 4 * q : 4 * q + 4, :].bitcast(I32))
         w1_raw.append(load_columns(w1, halves[1], "w1_raw1"))
         xw = keep.tile([P, T], I32, name="xw", align_bytes=64)
         nc.sync.dma_start(out=xw[:], in_=x_words[0].rearrange("p n t -> p (n t)").bitcast(I32))
-        two_t = load_list(two, "two_t")
         n1_t = load_list(n1, "n1_t")
         gn_t = keep.tile([P, PACK], F32, name="gn_t")
         nc.sync.dma_start(out=gn_t[:], in_=gn.rearrange("(p t) o -> p (t o)", t=PACK))
@@ -97,7 +97,7 @@ def tile_picked_lateflowbrms_none_p_kernel(
         def quantise(grouped, name):
             codes = keep.tile([P, S], U32, name=name + "_codes", align_bytes=64)
             scales = keep.tile([P, S], U8, name=name + "_sc", align_bytes=64)
-            nc.vector.quantize_mx(out=codes[:].bitcast(FP8X4), scales=scales[:], in_=grouped[:])
+            nc.vector.quantize_mx(out=codes[:].bitcast(FP8X4), scales=scales[:], in_=grouped)
             return codes, scales
 
         def product(acc, w, t, x, cols=slice(0, S)):
@@ -112,7 +112,7 @@ def tile_picked_lateflowbrms_none_p_kernel(
         w1_grouped = keep.tile([P, PACK * S], BF16, name="w1_grouped", align_bytes=64)
         for half in range(2):
             deal(nc.scalar.copy, w1_grouped, w1_raw[half], half * P // 2)
-        w1q = quantise(w1_grouped, "w1")
+        w1q = quantise(w1_grouped[:], "w1")
         xq_words = keep.tile([P, S], U32, name="xq_words", align_bytes=64)
         for half in range(2):
             nc.vector.tensor_copy(out=xq_words[:, halves[half]], in_=xw[:].bitcast(U32).indirect(offs_t[:, 16 * half : 16 * half + 16]))
@@ -134,7 +134,10 @@ def tile_picked_lateflowbrms_none_p_kernel(
                 product(acc, w1q, t, xq, cols)
                 nc.scalar.activation(out=sq_win[t][:, cols], in_=acc[:, cols], func=ACT.Square)
                 nc.scalar.activation(out=y_win[t][:, S:][:, cols], in_=acc[:, cols], func=ACT.Square)
-            nc.vector.tensor_tensor(out=s[:, t, :], in0=sq_win[t][:].indirect(n1_t[:]), in1=y_win[t][:, S:], op=ALU.add)
+            for acc, cols in y[t]:
+                nc.vector.tensor_tensor(
+                    out=s[:, t, cols], in0=sq_win[t][:].indirect(n1_t[:, cols.start // 16 : cols.stop // 16]), in1=y_win[t][:, S:][:, cols], op=ALU.add
+                )
         for t in range(PACK):
             for acc, cols in y[t]:
                 nc.scalar.activation(out=y_win[t][:, cols], in_=acc[:, cols], func=ACT.Copy, scale=gn_t[:, t : t + 1])
@@ -143,26 +146,44 @@ def tile_picked_lateflowbrms_none_p_kernel(
 
         w2_grouped = keep.tile([P, PACK * S], BF16, name="w2_grouped", align_bytes=64)
         deal(nc.scalar.copy, w2_grouped, w2_raw, 0)
-        zg = keep.tile([P, PACK * S], BF16, name="zg", align_bytes=64)
-        zg_view = zg[:].rearrange("p (c i t) -> p c t i", i=4, t=PACK)
+        staging = keep.tile([P, 6 * S], BF16, name="staging", align_bytes=64)
+        zg = staging[:, : PACK * S]
+        w3_grouped = staging[:, 2 * S :]
+        zg_view = zg.rearrange("p (c i t) -> p c t i", i=4, t=PACK)
         z_view = z[:].rearrange("p t (c i) -> p c t i", i=4)
-        nc.vector.tensor_copy(out=zg_view[:, :80], in_=z_view[:, :80])
-        nc.scalar.copy(out=zg_view[:, 80:], in_=z_view[:, 80:])
-        w2q = quantise(w2_grouped, "w2")
-        zq = quantise(zg, "z")
-        deal(nc.vector.tensor_copy, zg, w3_raw, 0)
-        w3q = quantise(zg, "w3")
+        nc.vector.tensor_copy(out=zg_view[:, :64], in_=z_view[:, :64])
+        nc.vector.tensor_copy(out=zg_view[:, 64:104], in_=z_view[:, 64:104])
+        nc.scalar.copy(out=zg_view[:, 104:], in_=z_view[:, 104:])
+        w2q = quantise(w2_grouped[:], "w2")
+        z_codes = keep.tile([P, S], U32, name="z_codes", align_bytes=64)
+        z_scales = keep.tile([P, S], U8, name="z_scales", align_bytes=64)
+        for cols in halves:
+            nc.vector.quantize_mx(out=z_codes[:, cols].bitcast(FP8X4), scales=z_scales[:, cols], in_=zg[:, PACK * cols.start : PACK * cols.stop])
+        zq = (z_codes, z_scales)
+        w3_dst = w3_grouped.rearrange("p (t m j) -> p m j t", t=PACK, j=PACK)
+        w3_src = w3_raw[:].rearrange("p j (m t) -> p m j t", t=PACK)
+        nc.scalar.copy(out=w3_dst[:, :, :, 2:], in_=w3_src[:, :, :, 2:])
+        nc.vector.tensor_copy(out=w3_dst[:, :, :, :2], in_=w3_src[:, :, :, :2])
+        w3q = quantise(w3_grouped, "w3")
 
         h, d = [], []
         for t in range(PACK):
-            h.append(psum.tile([P, S], F32, name="h%d" % t, tag="h%d" % t))
-            product(h[t], w2q, t, zq)
+            bank = psum.tile([P, S], F32, name="h%d" % t, tag="h%d" % t)
+            if t == 0:
+                early = psum.tile([P, S], F32, name="h_early", tag="yd3")
+                h.append([(early, halves[0]), (bank, halves[1])])
+            else:
+                h.append([(bank, slice(0, S))])
+            for acc, cols in h[t]:
+                product(acc, w2q, t, zq, cols)
         for t in range(PACK):
             d.append(psum.tile([P, S], F32, name="d%d" % t, tag="yd%d" % t))
             product(d[t], w3q, t, x2)
         for t in range(PACK):
-            nc.scalar.copy(out=sq_win[t][:, :S], in_=h[t][:])
-            nc.scalar.copy(out=d_win[t][:, S:], in_=h[t][:])
+            for acc, cols in h[t]:
+                nc.scalar.copy(out=sq_win[t][:, cols], in_=acc[:, cols])
+            for acc, cols in h[t]:
+                nc.scalar.copy(out=d_win[t][:, S:][:, cols], in_=acc[:, cols])
             nc.scalar.activation(out=d_win[t][:, :S], in_=d[t][:], func=ACT.Copy, scale=0.5)
 
         a = keep.tile([P, PACK, S], F32, name="a")
@@ -191,7 +212,10 @@ def tile_picked_lateflowbrms_none_p_kernel(
             nc.sync.dma_start(out=out_rows[:, t, :], in_=res[:, t, :])
 
         for t in range(PACK):
-            nc.vector.tensor_tensor(out=b[:, t, :], in0=sq_win[t][:].indirect(n4_t[:]), in1=d_win[t][:, S:], op=ALU.subtract)
+            for acc, cols in h[t]:
+                nc.vector.tensor_tensor(
+                    out=b[:, t, cols], in0=sq_win[t][:].indirect(n4_t[:, cols.start // 16 : cols.stop // 16]), in1=d_win[t][:, S:][:, cols], op=ALU.subtract
+                )
             nc.vector.tensor_tensor(out=a[:, t, :], in0=sq_win[t][:].indirect(n3_t[:]), in1=d_win[t][:, S:], op=ALU.subtract)
             if t < PACK - 1:
                 nc.vector.tensor_tensor(out=c[:, t, :], in0=d_win[t][:].indirect(n5_t[:]), in1=b[:, t, :], op=ALU.mult)

from contextlib import ExitStack

import concourse.mybir as mybir
from concourse.masks import make_identity

F32 = mybir.dt.float32
BF16 = mybir.dt.bfloat16
I32 = mybir.dt.int32
U32 = mybir.dt.uint32
U16 = mybir.dt.uint16
U8 = mybir.dt.uint8
FP8X4 = mybir.dt.float8_e4m3fn_x4
ACT = mybir.ActivationFunctionType
ALU = mybir.AluOpType

P = 128
PACK = 4
T = 2048
S = 512
HALF = S // 2
FLOPS = 3 * 2 * 512 * 512 * 512


def tile_picked_lateflowbrms_none_p_kernel(
    tc, x_words, x_scales, w1, gn, w2, w3, offs, n1, n2, two, n3, n4, n5, out
):
    nc = tc.nc
    with ExitStack() as ctx:
        keep = ctx.enter_context(tc.tile_pool(name="keep", bufs=1))
        psum = ctx.enter_context(tc.psum_pool(name="psum", bufs=1))

        def load_list(src, name):
            tile = keep.tile([P, S // 16], U16, name=name)
            nc.sync.dma_start(tile[:], src)
            return tile

        def load_weight(src, name):
            tile = keep.tile([P, PACK, S], F32, name=name)
            nc.sync.dma_start(out=tile[:], in_=src.rearrange("(p j) c -> p j c", j=PACK))
            return tile

        def load_columns(src, cols, name):
            tile = keep.tile([P, PACK, cols.stop - cols.start], F32, name=name)
            nc.sync.dma_start(out=tile[:], in_=src[:, cols].rearrange("(p j) c -> p j c", j=PACK))
            return tile

        halves = [slice(0, HALF), slice(HALF, S)]
        xs = keep.tile([P, T], U8, name="xs", align_bytes=64)
        nc.gpsimd.memset(xs[:].bitcast(I32), 0)
        warm_in = keep.tile([P, 1], F32, name="warm_in")
        warm_out = keep.tile([P, 1], F32, name="warm_out")
        nc.vector.memset(warm_in[:], 1.0)
        nc.scalar.activation(out=warm_out[:], in_=warm_in[:], func=ACT.Abs_reciprocal_sqrt)
        offs_t = load_list(offs, "offs_t")
        two_t = load_list(two, "two_t")
        w1_raw = [load_columns(w1, halves[0], "w1_raw0")]
        for q in range(4):
            nc.sync.dma_start(out=xs[32 * q : 32 * q + 4, :].bitcast(I32), in_=x_scales[0, 4 * q : 4 * q + 4, :].bitcast(I32))
        w1_raw.append(load_columns(w1, halves[1], "w1_raw1"))
        xw = keep.tile([P, T], I32, name="xw", align_bytes=64)
        nc.sync.dma_start(out=xw[:], in_=x_words[0].rearrange("p n t -> p (n t)").bitcast(I32))
        n1_t = load_list(n1, "n1_t")
        gn_t = keep.tile([P, PACK], F32, name="gn_t")
        nc.sync.dma_start(out=gn_t[:], in_=gn.rearrange("(p t) o -> p (t o)", t=PACK))
        n2_t = load_list(n2, "n2_t")
        w2_raw = load_weight(w2, "w2_raw")
        w3_raw = load_weight(w3, "w3_raw")
        n4_t = load_list(n4, "n4_t")
        n3_t = load_list(n3, "n3_t")
        n5_t = load_list(n5, "n5_t")

        sq_win = [keep.tile([P, 2 * S], F32, name="sq_win%d" % t) for t in range(PACK)]
        y_win = [keep.tile([P, 2 * S], F32, name="y_win%d" % t) for t in range(PACK)]
        d_win = [keep.tile([P, 2 * S], F32, name="d_win%d" % t) for t in range(PACK)]
        for t in range(PACK):
            nc.gpsimd.memset(sq_win[t][:, S:], 0.0)
        ident = keep.tile([P, P], F32, name="ident")
        make_identity(nc, ident[:])

        def pick_scales(lst, name):
            scales = keep.tile([P, S], U8, name=name, align_bytes=64)
            nc.vector.tensor_copy(out=scales[:], in_=xs[:].indirect(lst[:]))
            return scales

        def pick_words(lst, name):
            words = keep.tile([P, S], U32, name=name, align_bytes=64)
            nc.vector.tensor_copy(out=words[:], in_=xw[:].bitcast(U32).indirect(lst[:]))
            return words

        def deal(copy, grouped, raw, first):
            n = raw.shape[2] // PACK
            copy(
                out=grouped[:].rearrange("p (t m j) -> p m j t", t=PACK, j=PACK)[:, first : first + n],
                in_=raw[:].rearrange("p j (m t) -> p m j t", t=PACK),
            )

        def quantise(grouped, name):
            codes = keep.tile([P, S], U32, name=name + "_codes", align_bytes=64)
            scales = keep.tile([P, S], U8, name=name + "_sc", align_bytes=64)
            nc.vector.quantize_mx(out=codes[:].bitcast(FP8X4), scales=scales[:], in_=grouped)
            return codes, scales

        def product(acc, w, t, x, cols=slice(0, S)):
            m = slice(P * t, P * (t + 1))
            nc.tensor.matmul_mx(
                out=acc[:, cols], lhsT=w[0][:, m].bitcast(FP8X4), lhsT_scale=w[1][:, m],
                rhs=x[0][:, cols].bitcast(FP8X4), rhs_scale=x[1][:, cols], start=True, stop=True,
            )

        xq_scales = pick_scales(offs_t, "xq_scales")
        x2_scales = pick_scales(two_t, "x2_scales")
        w1_grouped = keep.tile([P, PACK * S], BF16, name="w1_grouped", align_bytes=64)
        for half in range(2):
            deal(nc.scalar.copy, w1_grouped, w1_raw[half], half * P // 2)
        w1q = quantise(w1_grouped[:], "w1")
        xq_words = keep.tile([P, S], U32, name="xq_words", align_bytes=64)
        for half in range(2):
            nc.vector.tensor_copy(out=xq_words[:, halves[half]], in_=xw[:].bitcast(U32).indirect(offs_t[:, 16 * half : 16 * half + 16]))
        xq = (xq_words, xq_scales)
        x2 = (pick_words(two_t, "x2_words"), x2_scales)

        s = keep.tile([P, PACK, S], F32, name="s")
        r = keep.tile([P, PACK, S], F32, name="r")
        z = keep.tile([P, PACK, S], F32, name="z")
        y = []
        for t in range(PACK):
            bank = psum.tile([P, S], F32, name="y%d" % t, tag="yd%d" % t)
            if t == 0:
                early = psum.tile([P, S], F32, name="y_early", tag="h0")
                y.append([(early, halves[0]), (bank, halves[1])])
            else:
                y.append([(bank, slice(0, S))])
            for acc, cols in y[t]:
                product(acc, w1q, t, xq, cols)
                nc.scalar.activation(out=sq_win[t][:, cols], in_=acc[:, cols], func=ACT.Square)
                nc.scalar.activation(out=y_win[t][:, S:][:, cols], in_=acc[:, cols], func=ACT.Square)
            for acc, cols in y[t]:
                nc.vector.tensor_tensor(
                    out=s[:, t, cols], in0=sq_win[t][:].indirect(n1_t[:, cols.start // 16 : cols.stop // 16]), in1=y_win[t][:, S:][:, cols], op=ALU.add
                )
        for t in range(PACK):
            for acc, cols in y[t]:
                nc.scalar.activation(out=y_win[t][:, cols], in_=acc[:, cols], func=ACT.Copy, scale=gn_t[:, t : t + 1])
            nc.scalar.activation(out=r[:, t, :], in_=s[:, t, :], func=ACT.Abs_reciprocal_sqrt, bias=0.25)
            nc.vector.tensor_tensor(out=z[:, t, :], in0=y_win[t][:].indirect(n2_t[:]), in1=r[:, t, :], op=ALU.mult)

        w2_grouped = keep.tile([P, PACK * S], BF16, name="w2_grouped", align_bytes=64)
        deal(nc.scalar.copy, w2_grouped, w2_raw, 0)
        staging = keep.tile([P, 6 * S], BF16, name="staging", align_bytes=64)
        zg = staging[:, : PACK * S]
        w3_grouped = staging[:, 2 * S :]
        zg_view = zg.rearrange("p (c i t) -> p c t i", i=4, t=PACK)
        z_view = z[:].rearrange("p t (c i) -> p c t i", i=4)
        nc.vector.tensor_copy(out=zg_view[:, :64], in_=z_view[:, :64])
        nc.vector.tensor_copy(out=zg_view[:, 64:104], in_=z_view[:, 64:104])
        nc.scalar.copy(out=zg_view[:, 104:], in_=z_view[:, 104:])
        w2q = quantise(w2_grouped[:], "w2")
        z_codes = keep.tile([P, S], U32, name="z_codes", align_bytes=64)
        z_scales = keep.tile([P, S], U8, name="z_scales", align_bytes=64)
        for cols in halves:
            nc.vector.quantize_mx(out=z_codes[:, cols].bitcast(FP8X4), scales=z_scales[:, cols], in_=zg[:, PACK * cols.start : PACK * cols.stop])
        zq = (z_codes, z_scales)
        w3_dst = w3_grouped.rearrange("p (t m j) -> p m j t", t=PACK, j=PACK)
        w3_src = w3_raw[:].rearrange("p j (m t) -> p m j t", t=PACK)
        nc.scalar.copy(out=w3_dst[:, :, :, 2:], in_=w3_src[:, :, :, 2:])
        nc.vector.tensor_copy(out=w3_dst[:, :, :, :2], in_=w3_src[:, :, :, :2])
        w3q = quantise(w3_grouped, "w3")

        h, d = [], []
        for t in range(PACK):
            bank = psum.tile([P, S], F32, name="h%d" % t, tag="h%d" % t)
            if t == 0:
                early = psum.tile([P, S], F32, name="h_early", tag="yd3")
                h.append([(early, halves[0]), (bank, halves[1])])
            else:
                h.append([(bank, slice(0, S))])
            for acc, cols in h[t]:
                product(acc, w2q, t, zq, cols)
        for t in range(PACK):
            d.append(psum.tile([P, S], F32, name="d%d" % t, tag="yd%d" % t))
            product(d[t], w3q, t, x2)
        for t in range(PACK):
            for acc, cols in h[t]:
                nc.scalar.copy(out=sq_win[t][:, cols], in_=acc[:, cols])
            for acc, cols in h[t]:
                nc.scalar.copy(out=d_win[t][:, S:][:, cols], in_=acc[:, cols])
            nc.scalar.activation(out=d_win[t][:, :S], in_=d[t][:], func=ACT.Copy, scale=0.5)

        a = keep.tile([P, PACK, S], F32, name="a")
        b = keep.tile([P, PACK, S], F32, name="b")
        c = keep.tile([P, PACK, S], F32, name="c")
        e = keep.tile([P, PACK, S], F32, name="e")
        res = keep.tile([P, PACK, S], F32, name="res")
        out_rows = out.rearrange("(p t) j -> p t j", t=PACK)

        def finish(t, cols):
            nc.vector.tensor_tensor(out=res[:, t, cols], in0=c[:, t, cols], in1=e[:, t, cols], op=ALU.add)
            nc.sync.dma_start(out=out_rows[:, t, cols], in_=res[:, t, cols])

        def finish_on_tensor(t):
            turned = psum.tile([P, S], F32, name="turned%d" % t, tag="h%d" % t)
            for k in range(PACK):
                cols = slice(P * k, P * (k + 1))
                nc.tensor.matmul(out=turned[:, cols], lhsT=c[:, t, cols], rhs=ident[:], is_transpose=True, start=True, stop=False)
                nc.tensor.matmul(out=turned[:, cols], lhsT=e[:, t, cols], rhs=ident[:], is_transpose=True, start=False, stop=True)
            nc.scalar.copy(out=a[:, t, :], in_=turned[:])
            back = psum.tile([P, S], F32, name="back%d" % t, tag="yd%d" % t)
            for k in range(PACK):
                cols = slice(P * k, P * (k + 1))
                nc.tensor.transpose(back[:, cols], a[:, t, cols], ident[:])
            nc.scalar.copy(out=res[:, t, :], in_=back[:])
            nc.sync.dma_start(out=out_rows[:, t, :], in_=res[:, t, :])

        for t in range(PACK):
            for acc, cols in h[t]:
                nc.vector.tensor_tensor(
                    out=b[:, t, cols], in0=sq_win[t][:].indirect(n4_t[:, cols.start // 16 : cols.stop // 16]), in1=d_win[t][:, S:][:, cols], op=ALU.subtract
                )
            nc.vector.tensor_tensor(out=a[:, t, :], in0=sq_win[t][:].indirect(n3_t[:]), in1=d_win[t][:, S:], op=ALU.subtract)
            if t < PACK - 1:
                nc.vector.tensor_tensor(out=c[:, t, :], in0=d_win[t][:].indirect(n5_t[:]), in1=b[:, t, :], op=ALU.mult)
                nc.vector.tensor_tensor(out=e[:, t, :], in0=d[t][:], in1=a[:, t, :], op=ALU.mult)
                finish_on_tensor(t)
        t = PACK - 1
        nc.vector.tensor_tensor(out=c[:, t, halves[0]], in0=d_win[t][:].indirect(n5_t[:, 0:16]), in1=b[:, t, halves[0]], op=ALU.mult)
        nc.vector.tensor_tensor(out=e[:, t, :], in0=d[t][:], in1=a[:, t, :], op=ALU.mult)
        nc.vector.tensor_tensor(out=c[:, t, halves[1]], in0=d_win[t][:].indirect(n5_t[:, 16:32]), in1=b[:, t, halves[1]], op=ALU.mult)
        finish(t, halves[0])
        finish(t, halves[1])
